import numpy as np
import ml_dtypes


def mxq(x, axis, fmt="e4m3"):
    dtype, down = {"e4m3": (ml_dtypes.float8_e4m3fn, 7), "e5m2": (ml_dtypes.float8_e5m2, 14)}[fmt]
    v = np.moveaxis(np.asarray(x, np.float32).astype(ml_dtypes.bfloat16).astype(np.float64), axis, -1)
    blocks = v.reshape(v.shape[:-1] + (-1, 32))
    amax = np.abs(blocks).max(-1, keepdims=True)
    byte = np.maximum(np.where(amax > 0, np.frexp(amax)[1] - 1 + 127, 0) - down, 1)
    scale = np.exp2(byte - 127.0)
    codes = (blocks / scale).astype(np.float32).astype(dtype).astype(np.float64)
    return np.moveaxis((codes * scale).reshape(v.shape), -1, axis)


WIDE = False


def mx_kscale(k):
    if not WIDE:
        return np.ones(k)
    levels = np.array([10, -10, 5, -5, 0])
    if k % 512:
        return np.exp2(np.random.permutation(np.resize(levels, k // 32))).repeat(32)
    a = np.empty((k // 512, 16))
    for p in range(k // 512):
        a[p, :8] = np.random.permutation(np.resize(levels, 8))
        for g in range(8):
            far = levels[np.abs(levels - a[p, g]) >= 10]
            a[p, g + 8] = far[np.random.randint(len(far))]
    return np.exp2(a.ravel()).repeat(32)


def f64(x):
    return np.asarray(x).astype(np.float64)


def striped(idx):
    return np.tile(np.asarray(idx).reshape(-1, 16).T, (8, 1)).astype(np.uint16)


def unstriped(offs):
    return offs[:16].T.reshape(-1).astype(np.int64)


E2M1 = np.array([0.0, 0.5, 1.0, 1.5, 2.0, 3.0, 4.0, 6.0, -0.0, -0.5, -1.0, -1.5, -2.0, -3.0, -4.0, -6.0])


def pack_weight(w, fmt):
    k, n = w.shape
    w = f64(np.asarray(w, np.float32).astype(ml_dtypes.bfloat16)).reshape(k // 32, 32, n)
    amax = np.abs(w).max(1)
    if fmt == "e4m3":
        byte = np.frexp(amax)[1] - 1 + 127 - 7
    else:
        mant, ex = np.frexp(amax / 6.0)
        byte = np.where(mant > 0.5, ex, ex - 1) + 127
    byte = np.clip(np.where(amax > 0, byte, 1), 1, 254)
    scaled = (w * np.exp2(127.0 - byte)[:, None, :]).reshape(k, n).astype(np.float32)
    by_word = np.ascontiguousarray(scaled.reshape(k // 512, 128, 4, n).transpose(0, 1, 3, 2))
    if fmt == "e4m3":
        words = by_word.astype(ml_dtypes.float8_e4m3fn).view(np.uint8)
    else:
        c = by_word.astype(ml_dtypes.float4_e2m1fn).view(np.uint8) & 0xF
        words = (c[..., 0::2] | (c[..., 1::2] << 4)).reshape(k // 512, 128, 2 * n)
    return np.ascontiguousarray(words), np.ascontiguousarray(byte.astype(np.uint8).reshape(k // 512, 16, n))


def unpack_weight(words, scales, fmt):
    g, _, n = scales.shape
    words = np.ascontiguousarray(words).reshape(g, 128, n, -1)
    if fmt == "e4m3":
        vals = words.view(ml_dtypes.float8_e4m3fn).astype(np.float64)
    else:
        nib = np.empty((g, 128, n, 4), np.uint8)
        nib[..., 0::2] = words & 0xF
        nib[..., 1::2] = words >> 4
        vals = E2M1[nib]
    vals = vals * np.repeat(np.exp2(scales.astype(np.float64) - 127.0), 8, axis=1)[..., None]
    return vals.transpose(0, 1, 3, 2).reshape(g * 512, n)


def bf(x):
    return np.asarray(x, np.float32).astype(ml_dtypes.bfloat16)


def planes(Y):
    r, m = Y.shape
    b = f64(bf(Y)).reshape(r // 32, 32, m)
    amax = np.abs(b).max(1)
    byte = np.clip(np.where(amax > 0, np.frexp(amax)[1] - 1 + 127 - 7, 1), 1, 254)
    codes = (b * np.exp2(127.0 - byte)[:, None, :]).reshape(r, m).astype(np.float32).astype(ml_dtypes.float8_e4m3fn).view(np.uint8)
    words = codes.reshape(r // 512, 128, 4, m).transpose(0, 1, 3, 2)
    return np.ascontiguousarray(words), np.ascontiguousarray(byte.astype(np.uint8).reshape(r // 512, 16, m))


D, T, I, J, U, E, M, C = 512, 2048, 512, 256, 1024, 512, 1024, 512


def setup_inputs():
    n = np.random.standard_normal
    idx = np.random.permutation(T)[:I]
    idx2 = np.random.permutation(U)[:J]
    idx3 = np.random.permutation(M)[:J]
    fd = mx_kscale(D)
    fi = mx_kscale(I)
    fc = mx_kscale(C)
    ti = np.ones(T)
    ti[idx] = fi
    keysp = pack_weight(n((D, T)) / fd[:, None], "e2m1")
    return {
        "keys_words": keysp[0],
        "keys_scales": keysp[1],
        "notes": (n((D, U)) * 1.0 / np.sqrt(D) * fd[:, None]).astype(np.float32),
        "rowf": (np.random.uniform(0.02, 0.08, (I, 1)) * fi[:, None]).astype(np.float32),
        "vals": (n((E, T)) / ti).astype(np.float32),
        "wm": (n((C, E)) * 1.0 / np.sqrt(C) * fc[:, None]).astype(np.float32),
        "mstore": (n((C, M)) / fc[:, None]).astype(np.float32),
        "offs": striped(idx),
        "offs2": striped(idx2),
        "offs3": striped(idx3),
    }


def reference(keys_words, keys_scales, notes, rowf, vals, wm, mstore, offs, offs2, offs3):
    idx = unstriped(offs)
    idx2 = unstriped(offs2)
    idx3 = unstriped(offs3)
    keysu = unpack_weight(keys_words, keys_scales, "e2m1")
    keysidxg = keysu[:, idx]
    notesidx2q = mxq(f64(notes)[:, idx2], 0, "e4m3")
    g9 = keysidxg.T @ notesidx2q
    g0 = np.maximum(g9, 0.0)
    gr1 = g0 * f64(rowf)
    vt1 = f64(vals)[:, idx].T
    vt1q = mxq(vt1, 0, "e4m3")
    gr1q = mxq(gr1, 0, "e4m3")
    o = vt1q.T @ gr1q
    wmq = mxq(f64(wm), 0, "e4m3")
    mstoreq = mxq(f64(mstore), 0, "e4m3")
    me = wmq.T @ mstoreq
    y = o * me[:, idx3]
    words, scales = planes(y)
    return y, words, scales

@@ -1,0 +1,191 @@
+from contextlib import ExitStack
+
+import concourse.mybir as mybir
+from concourse.masks import make_identity
+
+D, T, I, J, U, E, M, C = 512, 2048, 512, 256, 1024, 512, 1024, 512
+FLOPS = 2 * D * I * J + 2 * I * E * J + 2 * C * E * M
+
+F32 = mybir.dt.float32
+BF16 = mybir.dt.bfloat16
+I32 = mybir.dt.int32
+U32 = mybir.dt.uint32
+U16 = mybir.dt.uint16
+U8 = mybir.dt.uint8
+FP8X4 = mybir.dt.float8_e4m3fn_x4
+FP4X4 = mybir.dt.float4_e2m1fn_x4
+COPY = mybir.ActivationFunctionType.Copy
+MULT = mybir.AluOpType.mult
+MAX = mybir.AluOpType.max
+
+P = 128
+PACK = 4
+BANK = 512
+
+
+def tile_attend_tab_plain_gains_pl_kernel(
+    tc, keys_words, keys_scales, notes, rowf, vals, wm, mstore, offs, offs2, offs3, out_0, out_1, out_2
+):
+    nc = tc.nc
+    with ExitStack() as ctx:
+        sb = ctx.enter_context(tc.tile_pool(name="sb", bufs=1))
+        ps = ctx.enter_context(tc.psum_pool(name="ps", bufs=2))
+
+        def tile(name, shape, dtype):
+            return sb.tile(shape, dtype, name=name, align_bytes=64)
+
+        def quantise(name, grouped, width):
+            codes = tile(name + "_codes", [P, width], U32)
+            scales = tile(name + "_scales", [P, width], U8)
+            nc.vector.quantize_mx(out=codes[:].bitcast(FP8X4), scales=scales[:], in_=grouped)
+            return codes, scales
+
+        def interleave(grouped, planes):
+            nc.vector.tensor_copy(
+                out=grouped.rearrange("p (c i t) -> p c t i", i=PACK, t=PACK),
+                in_=planes.rearrange("p t (c i) -> p c t i", i=PACK),
+            )
+
+        idx = sb.tile([P, I // 16], U16, name="idx")
+        idx2 = sb.tile([P, J // 16], U16, name="idx2")
+        idx3 = sb.tile([P, J // 16], U16, name="idx3")
+        key_words = tile("key_words", [P, T], U16)
+        key_bytes = tile("key_bytes", [P, T], U8)
+        row_factor = tile("row_factor", [P, PACK], F32)
+        wm_raw = tile("wm_raw", [P, PACK, E], F32)
+        store_raw = [tile(f"store_raw{h}", [P, PACK, BANK], F32) for h in range(M // BANK)]
+        note_pool = [tile(f"note_pool{t}", [P, U], F32) for t in range(PACK)]
+        val_pool = [tile(f"val_pool{t}", [P, T], F32) for t in range(PACK)]
+
+        nc.vector.memset(key_bytes[:].bitcast(I32), 0)
+        nc.sync.dma_start(idx[:], offs)
+        nc.sync.dma_start(key_words[:].bitcast(I32), keys_words[0].bitcast(I32))
+        for q in range(4):
+            nc.scalar.dma_start(
+                key_bytes[32 * q : 32 * q + 4, :].bitcast(I32), keys_scales[0, 4 * q : 4 * q + 4, :].bitcast(I32)
+            )
+        nc.sync.dma_start(wm_raw[:], wm.rearrange("(p t) e -> p t e", t=PACK))
+        store_rows = mstore.rearrange("(p t) m -> p t m", t=PACK)
+        for h in range(M // BANK):
+            nc.sync.dma_start(store_raw[h][:], store_rows[:, :, h * BANK : (h + 1) * BANK])
+        nc.scalar.dma_start(row_factor[:], rowf.rearrange("(p t) one -> p (t one)", t=PACK))
+        nc.sync.dma_start(idx2[:], offs2)
+        nc.sync.dma_start(idx3[:], offs3)
+        note_rows = notes.rearrange("(p t) u -> p t u", t=PACK)
+        for t in range(PACK):
+            nc.sync.dma_start(note_pool[t][:], note_rows[:, t, :])
+        val_rows = vals.rearrange("(p t) n -> p t n", t=PACK)
+        for t in range(PACK):
+            nc.sync.dma_start(val_pool[t][:], val_rows[:, t, :])
+
+        identity = tile("identity", [P, P], F32)
+        make_identity(nc, identity[:])
+
+        picked_words = tile("picked_words", [P, I], U16)
+        nc.vector.tensor_copy(picked_words[:], key_words[:].indirect(idx[:]))
+        dealt_bytes = tile("dealt_bytes", [P, PACK, P], U8)
+        nc.vector.tensor_copy(dealt_bytes[:].rearrange("p t s -> p s t"), key_bytes[:].indirect(idx[:]))
+        dealt_words = tile("dealt_words", [P, PACK, P], U16)
+        nc.vector.tensor_copy(
+            dealt_words[:].rearrange("p t s -> p s t"), picked_words[:].rearrange("p (s t) -> p s t", t=PACK)
+        )
+
+        wm_grouped = tile("wm_grouped", [P, E * PACK], BF16)
+        nc.scalar.copy(
+            out=wm_grouped[:].rearrange("p (t s r) -> p s r t", t=PACK, r=PACK),
+            in_=wm_raw[:].rearrange("p r (s t) -> p s r t", t=PACK),
+        )
+        wm_codes, wm_scales = quantise("wm", wm_grouped[:], E)
+        memories = [tile(f"memories{t}", [P, M], F32) for t in range(PACK)]
+        for h in range(M // BANK):
+            store_grouped = tile(f"store_grouped{h}", [P, BANK * PACK], BF16)
+            interleave(store_grouped[:], store_raw[h][:])
+            store_codes, store_scales = quantise(f"store{h}", store_grouped[:], BANK)
+            for t in range(PACK):
+                me_bank = ps.tile([P, BANK], F32, name="me_bank")
+                nc.tensor.matmul_mx(
+                    out=me_bank[:],
+                    lhsT=wm_codes[:, t * P : (t + 1) * P].bitcast(FP8X4),
+                    lhsT_scale=wm_scales[:, t * P : (t + 1) * P],
+                    rhs=store_codes[:].bitcast(FP8X4),
+                    rhs_scale=store_scales[:],
+                    start=True,
+                    stop=True,
+                )
+                nc.scalar.copy(memories[t][:, h * BANK : (h + 1) * BANK], me_bank[:])
+        picked_me = [tile(f"picked_me{t}", [P, J], F32) for t in range(PACK)]
+        for t in range(PACK):
+            nc.scalar.activation(picked_me[t][:], memories[t][:].indirect(idx3[:]), COPY)
+
+        picked_notes = tile("picked_notes", [P, PACK, J], BF16)
+        for t in range(PACK):
+            nc.vector.tensor_copy(picked_notes[:, t, :], note_pool[t][:].indirect(idx2[:]))
+        notes_grouped = tile("notes_grouped", [P, J * PACK], BF16)
+        interleave(notes_grouped[:], picked_notes[:])
+        note_codes, note_scales = quantise("notes", notes_grouped[:], J)
+        table_grouped = tile("table_grouped", [P, J * PACK], BF16)
+        for h in range(J // P):
+            table_bank = ps.tile([P, PACK, P], F32, name="table_bank")
+            for t in range(PACK):
+                nc.tensor.matmul_mx(
+                    out=table_bank[:, t, :],
+                    lhsT=dealt_words[:, t, :].bitcast(FP4X4),
+                    lhsT_scale=dealt_bytes[:, t, :],
+                    rhs=note_codes[:, h * P : (h + 1) * P].bitcast(FP8X4),
+                    rhs_scale=note_scales[:, h * P : (h + 1) * P],
+                    start=True,
+                    stop=True,
+                )
+            nc.vector.scalar_tensor_tensor(
+                out=table_grouped[:, h * P * PACK : (h + 1) * P * PACK].rearrange("p (j t) -> p j t", t=PACK),
+                in0=table_bank[:].rearrange("p t j -> p j t"),
+                scalar=0.0,
+                in1=row_factor[:].unsqueeze(1).to_broadcast([P, P, PACK]),
+                op0=MAX,
+                op1=MULT,
+            )
+        table_codes, table_scales = quantise("table", table_grouped[:], J)
+
+        y = tile("y", [P, PACK, J], F32)
+        out_rows = out_0.rearrange("(p t) j -> p t j", t=PACK)
+        for t in range(PACK):
+            picked_vals = tile(f"picked_vals{t}", [P, I], BF16)
+            if t < PACK - 1:
+                nc.scalar.activation(picked_vals[:], val_pool[t][:].indirect(idx[:]), COPY)
+            else:
+                half, cols = I // 2, I // 32
+                nc.scalar.activation(picked_vals[:, :half], val_pool[t][:].indirect(idx[:, :cols]), COPY)
+                nc.vector.tensor_copy(picked_vals[:, half:], val_pool[t][:].indirect(idx[:, cols:]))
+            pairs = picked_vals[:].bitcast(F32)
+            turn_bank = ps.tile([P, 2, P], F32, name="turn_bank")
+            for u in range(2):
+                nc.tensor.transpose(turn_bank[:, u, :], pairs[:, u : I // 2 : 2], identity[:])
+            vals_grouped = tile(f"vals_grouped{t}", [P, P * PACK], BF16)
+            leave_bank = nc.vector.tensor_copy if t < PACK - 1 else nc.scalar.copy
+            leave_bank(
+                vals_grouped[:].bitcast(F32).rearrange("p (e u) -> p e u", u=2),
+                turn_bank[:].rearrange("p u e -> p e u"),
+            )
+            val_codes, val_scales = quantise(f"vals{t}", vals_grouped[:], P)
+            o_bank = ps.tile([P, J], F32, name="o_bank")
+            nc.tensor.matmul_mx(
+                out=o_bank[:],
+                lhsT=val_codes[:].bitcast(FP8X4),
+                lhsT_scale=val_scales[:],
+                rhs=table_codes[:].bitcast(FP8X4),
+                rhs_scale=table_scales[:],
+                start=True,
+                stop=True,
+            )
+            nc.vector.tensor_tensor(y[:, t, :], o_bank[:], picked_me[t][:], MULT)
+            if t == PACK - 2:
+                nc.sync.dma_start(out_rows[:, : PACK - 1, :], y[:, : PACK - 1, :])
+        nc.sync.dma_start(out_rows[:, PACK - 1, :], y[:, PACK - 1, :])
+
+        y_grouped = tile("y_grouped", [P, J * PACK], BF16)
+        interleave(y_grouped[:], y[:])
+        y_codes, y_scales = quantise("y", y_grouped[:], J)
+        nc.sync.dma_start(out_1[0].rearrange("p c r -> p (c r)").bitcast(I32), y_codes[:].bitcast(I32))
+        for q in range(4):
+            queue = nc.scalar if q % 2 == 0 else nc.sync
+            queue.dma_start(out_2[0, 4 * q : 4 * q + 4, :].bitcast(I32), y_scales[32 * q : 32 * q + 4, :].bitcast(I32))

@@ -31,17 +31,23 @@ def tile_attend_tab_plain_gains_pl_kernel(
         sb = ctx.enter_context(tc.tile_pool(name="sb", bufs=1))
         ps = ctx.enter_context(tc.psum_pool(name="ps", bufs=2))
 
-        def tile(name, shape, dtype):
-            return sb.tile(shape, dtype, name=name, align_bytes=64)
+        def tile(name, shape, dtype, tag=None):
+            return sb.tile(shape, dtype, name=name, tag=tag or name, align_bytes=64)
 
-        def quantise(name, grouped, width):
+        def quantise(name, grouped, width, parts=1):
             codes = tile(name + "_codes", [P, width], U32)
             scales = tile(name + "_scales", [P, width], U8)
-            nc.vector.quantize_mx(out=codes[:].bitcast(FP8X4), scales=scales[:], in_=grouped)
+            step = width // parts
+            for c in range(0, width, step):
+                nc.vector.quantize_mx(
+                    out=codes[:, c : c + step].bitcast(FP8X4),
+                    scales=scales[:, c : c + step],
+                    in_=grouped[:, c * PACK : (c + step) * PACK],
+                )
             return codes, scales
 
-        def interleave(grouped, planes):
-            nc.vector.tensor_copy(
+        def interleave(grouped, planes, copy=nc.vector.tensor_copy):
+            copy(
                 out=grouped.rearrange("p (c i t) -> p c t i", i=PACK, t=PACK),
                 in_=planes.rearrange("p t (c i) -> p c t i", i=PACK),
             )
@@ -61,7 +67,7 @@ def tile_attend_tab_plain_gains_pl_kernel(
         nc.sync.dma_start(idx[:], offs)
         nc.sync.dma_start(key_words[:].bitcast(I32), keys_words[0].bitcast(I32))
         for q in range(4):
-            nc.scalar.dma_start(
+            nc.sync.dma_start(
                 key_bytes[32 * q : 32 * q + 4, :].bitcast(I32), keys_scales[0, 4 * q : 4 * q + 4, :].bitcast(I32)
             )
         nc.sync.dma_start(wm_raw[:], wm.rearrange("(p t) e -> p t e", t=PACK))
@@ -91,18 +97,23 @@ def tile_attend_tab_plain_gains_pl_kernel(
         )
 
         wm_grouped = tile("wm_grouped", [P, E * PACK], BF16)
-        nc.scalar.copy(
+        nc.vector.tensor_copy(
             out=wm_grouped[:].rearrange("p (t s r) -> p s r t", t=PACK, r=PACK),
             in_=wm_raw[:].rearrange("p r (s t) -> p s r t", t=PACK),
         )
         wm_codes, wm_scales = quantise("wm", wm_grouped[:], E)
         memories = [tile(f"memories{t}", [P, M], F32) for t in range(PACK)]
         for h in range(M // BANK):
-            store_grouped = tile(f"store_grouped{h}", [P, BANK * PACK], BF16)
-            interleave(store_grouped[:], store_raw[h][:])
+            store_grouped = tile(f"store_grouped{h}", [P, BANK * PACK], BF16, tag="store_grouped")
+            if h == 0:
+                cut = BANK // 2
+                interleave(store_grouped[:, : cut * PACK], store_raw[h][:, :, :cut], nc.scalar.copy)
+                interleave(store_grouped[:, cut * PACK :], store_raw[h][:, :, cut:])
+            else:
+                interleave(store_grouped[:], store_raw[h][:])
             store_codes, store_scales = quantise(f"store{h}", store_grouped[:], BANK)
             for t in range(PACK):
-                me_bank = ps.tile([P, BANK], F32, name="me_bank")
+                me_bank = ps.tile([P, BANK], F32, name="me_bank", bufs=4)
                 nc.tensor.matmul_mx(
                     out=me_bank[:],
                     lhsT=wm_codes[:, t * P : (t + 1) * P].bitcast(FP8X4),
@@ -113,19 +124,20 @@ def tile_attend_tab_plain_gains_pl_kernel(
                     stop=True,
                 )
                 nc.scalar.copy(memories[t][:, h * BANK : (h + 1) * BANK], me_bank[:])
-        picked_me = [tile(f"picked_me{t}", [P, J], F32) for t in range(PACK)]
+        picked_me = [tile(f"picked_me{a}", [P, 2, J], F32) for a in range(PACK // 2)]
         for t in range(PACK):
-            nc.scalar.activation(picked_me[t][:], memories[t][:].indirect(idx3[:]), COPY)
+            nc.scalar.activation(picked_me[t // 2][:, t % 2, :], memories[t][:].indirect(idx3[:]), COPY)
 
-        picked_notes = tile("picked_notes", [P, PACK, J], BF16)
+        picked_notes = tile("picked_notes", [P, PACK, J], BF16, tag="store_grouped")
         for t in range(PACK):
             nc.vector.tensor_copy(picked_notes[:, t, :], note_pool[t][:].indirect(idx2[:]))
         notes_grouped = tile("notes_grouped", [P, J * PACK], BF16)
-        interleave(notes_grouped[:], picked_notes[:])
-        note_codes, note_scales = quantise("notes", notes_grouped[:], J)
+        for h in range(J // P):
+            interleave(notes_grouped[:, h * P * PACK : (h + 1) * P * PACK], picked_notes[:, :, h * P : (h + 1) * P])
+        note_codes, note_scales = quantise("notes", notes_grouped[:], J, parts=J // P)
         table_grouped = tile("table_grouped", [P, J * PACK], BF16)
         for h in range(J // P):
-            table_bank = ps.tile([P, PACK, P], F32, name="table_bank")
+            table_bank = ps.tile([P, PACK, P], F32, name="table_bank", tag=f"shared{h}", bufs=1)
             for t in range(PACK):
                 nc.tensor.matmul_mx(
                     out=table_bank[:, t, :],
@@ -144,30 +156,39 @@ def tile_attend_tab_plain_gains_pl_kernel(
                 op0=MAX,
                 op1=MULT,
             )
-        table_codes, table_scales = quantise("table", table_grouped[:], J)
+        table_codes, table_scales = quantise("table", table_grouped[:], J, parts=J // P)
 
-        y = tile("y", [P, PACK, J], F32)
-        out_rows = out_0.rearrange("(p t) j -> p t j", t=PACK)
-        for t in range(PACK):
-            picked_vals = tile(f"picked_vals{t}", [P, I], BF16)
+        def gather_values(t):
+            picked_vals = tile(f"picked_vals{t}", [P, I], BF16, tag=f"memories{t}" if t < PACK - 1 else "vals_grouped1")
             if t < PACK - 1:
                 nc.scalar.activation(picked_vals[:], val_pool[t][:].indirect(idx[:]), COPY)
             else:
                 half, cols = I // 2, I // 32
                 nc.scalar.activation(picked_vals[:, :half], val_pool[t][:].indirect(idx[:, :cols]), COPY)
                 nc.vector.tensor_copy(picked_vals[:, half:], val_pool[t][:].indirect(idx[:, cols:]))
+            return picked_vals
+
+        def turn_values(t, picked_vals):
             pairs = picked_vals[:].bitcast(F32)
-            turn_bank = ps.tile([P, 2, P], F32, name="turn_bank")
+            turn_bank = ps.tile([P, 2, P], F32, name="turn_bank", tag=f"shared{t % 2}", bufs=1)
             for u in range(2):
                 nc.tensor.transpose(turn_bank[:, u, :], pairs[:, u : I // 2 : 2], identity[:])
-            vals_grouped = tile(f"vals_grouped{t}", [P, P * PACK], BF16)
+            vals_grouped = tile(f"vals_grouped{t}", [P, P * PACK], BF16, tag="val_pool3" if t == 2 else None)
             leave_bank = nc.vector.tensor_copy if t < PACK - 1 else nc.scalar.copy
             leave_bank(
                 vals_grouped[:].bitcast(F32).rearrange("p (e u) -> p e u", u=2),
                 turn_bank[:].rearrange("p u e -> p e u"),
             )
-            val_codes, val_scales = quantise(f"vals{t}", vals_grouped[:], P)
-            o_bank = ps.tile([P, J], F32, name="o_bank")
+            return vals_grouped
+
+        y = tile("y", [P, PACK, J], F32)
+        out_rows = out_0.rearrange("(p t) j -> p t j", t=PACK)
+        y_grouped = tile("y_grouped", [P, J * PACK], BF16)
+        y_places = y_grouped[:].rearrange("p (c i t) -> p c t i", i=PACK, t=PACK)
+        y_planes = y[:].rearrange("p t (c i) -> p c t i", i=PACK)
+
+        def multiply_values(t, val_codes, val_scales, bank_tag):
+            o_bank = ps.tile([P, J], F32, name="o_bank", tag=bank_tag, bufs=1)
             nc.tensor.matmul_mx(
                 out=o_bank[:],
                 lhsT=val_codes[:].bitcast(FP8X4),
@@ -177,13 +198,28 @@ def tile_attend_tab_plain_gains_pl_kernel(
                 start=True,
                 stop=True,
             )
-            nc.vector.tensor_tensor(y[:, t, :], o_bank[:], picked_me[t][:], MULT)
-            if t == PACK - 2:
-                nc.sync.dma_start(out_rows[:, : PACK - 1, :], y[:, : PACK - 1, :])
-        nc.sync.dma_start(out_rows[:, PACK - 1, :], y[:, PACK - 1, :])
+            nc.vector.tensor_tensor(y[:, t, :], o_bank[:], picked_me[t // 2][:, t % 2, :], MULT)
 
-        y_grouped = tile("y_grouped", [P, J * PACK], BF16)
-        interleave(y_grouped[:], y[:])
+        def quantise_values(t, vals_grouped):
+            return quantise(f"vals{t}", vals_grouped[:], P)
+
+        vals0 = quantise_values(0, turn_values(0, gather_values(0)))
+        vals1 = quantise_values(1, turn_values(1, gather_values(1)))
+        multiply_values(0, *vals0, "o_first")
+        picked2 = gather_values(2)
+        picked3 = gather_values(3)
+        grouped2 = turn_values(2, picked2)
+        grouped3 = turn_values(3, picked3)
+        vals2 = quantise_values(2, grouped2)
+        vals3 = quantise_values(3, grouped3)
+        multiply_values(1, *vals1, "shared0")
+        nc.scalar.copy(y_places[:, :, 0:2, :], y_planes[:, :, 0:2, :])
+        multiply_values(2, *vals2, "shared1")
+        nc.sync.dma_start(out_rows[:, 0:3, :], y[:, 0:3, :])
+        multiply_values(3, *vals3, "o_last")
+        nc.sync.dma_start(out_rows[:, 3, :], y[:, 3, :])
+
+        nc.vector.tensor_copy(y_places[:, :, 2:4, :], y_planes[:, :, 2:4, :])
         y_codes, y_scales = quantise("y", y_grouped[:], J)
         nc.sync.dma_start(out_1[0].rearrange("p c r -> p (c r)").bitcast(I32), y_codes[:].bitcast(I32))
         for q in range(4):

@@ -64,12 +64,10 @@ def tile_attend_tab_plain_gains_pl_kernel(
         val_pool = [tile(f"val_pool{t}", [P, T], F32) for t in range(PACK)]
 
         nc.vector.memset(key_bytes[:].bitcast(I32), 0)
-        nc.sync.dma_start(idx[:], offs)
         nc.sync.dma_start(key_words[:].bitcast(I32), keys_words[0].bitcast(I32))
-        for q in range(4):
-            nc.sync.dma_start(
-                key_bytes[32 * q : 32 * q + 4, :].bitcast(I32), keys_scales[0, 4 * q : 4 * q + 4, :].bitcast(I32)
-            )
+        nc.sync.dma_start(idx[:], offs)
+        for r in range(4):
+            nc.sync.dma_start(key_bytes[r:P:32, :].bitcast(I32), keys_scales[0, r:16:4, :].bitcast(I32))
         nc.sync.dma_start(wm_raw[:], wm.rearrange("(p t) e -> p t e", t=PACK))
         store_rows = mstore.rearrange("(p t) m -> p t m", t=PACK)
         for h in range(M // BANK):
@@ -113,7 +111,7 @@ def tile_attend_tab_plain_gains_pl_kernel(
                 interleave(store_grouped[:], store_raw[h][:])
             store_codes, store_scales = quantise(f"store{h}", store_grouped[:], BANK)
             for t in range(PACK):
-                me_bank = ps.tile([P, BANK], F32, name="me_bank", bufs=4)
+                me_bank = ps.tile([P, BANK], F32, name="me_bank", bufs=3)
                 nc.tensor.matmul_mx(
                     out=me_bank[:],
                     lhsT=wm_codes[:, t * P : (t + 1) * P].bitcast(FP8X4),
@@ -124,9 +122,6 @@ def tile_attend_tab_plain_gains_pl_kernel(
                     stop=True,
                 )
                 nc.scalar.copy(memories[t][:, h * BANK : (h + 1) * BANK], me_bank[:])
-        picked_me = [tile(f"picked_me{a}", [P, 2, J], F32) for a in range(PACK // 2)]
-        for t in range(PACK):
-            nc.scalar.activation(picked_me[t // 2][:, t % 2, :], memories[t][:].indirect(idx3[:]), COPY)
 
         picked_notes = tile("picked_notes", [P, PACK, J], BF16, tag="store_grouped")
         for t in range(PACK):
@@ -159,7 +154,7 @@ def tile_attend_tab_plain_gains_pl_kernel(
         table_codes, table_scales = quantise("table", table_grouped[:], J, parts=J // P)
 
         def gather_values(t):
-            picked_vals = tile(f"picked_vals{t}", [P, I], BF16, tag=f"memories{t}" if t < PACK - 1 else "vals_grouped1")
+            picked_vals = tile(f"picked_vals{t}", [P, I], BF16, tag=("memories1", "memories2", "memories3", "vals_grouped1")[t])
             if t < PACK - 1:
                 nc.scalar.activation(picked_vals[:], val_pool[t][:].indirect(idx[:]), COPY)
             else:
@@ -187,24 +182,34 @@ def tile_attend_tab_plain_gains_pl_kernel(
         y_places = y_grouped[:].rearrange("p (c i t) -> p c t i", i=PACK, t=PACK)
         y_planes = y[:].rearrange("p t (c i) -> p c t i", i=PACK)
 
-        def multiply_values(t, val_codes, val_scales, bank_tag):
-            o_bank = ps.tile([P, J], F32, name="o_bank", tag=bank_tag, bufs=1)
+        def multiply_values(t, val_codes, val_scales, bank_tag, cols=slice(0, J)):
+            o_bank = ps.tile([P, cols.stop - cols.start], F32, name="o_bank", tag=bank_tag, bufs=1)
             nc.tensor.matmul_mx(
                 out=o_bank[:],
                 lhsT=val_codes[:].bitcast(FP8X4),
                 lhsT_scale=val_scales[:],
-                rhs=table_codes[:].bitcast(FP8X4),
-                rhs_scale=table_scales[:],
+                rhs=table_codes[:, cols].bitcast(FP8X4),
+                rhs_scale=table_scales[:, cols],
                 start=True,
                 stop=True,
             )
-            nc.vector.tensor_tensor(y[:, t, :], o_bank[:], picked_me[t // 2][:, t % 2, :], MULT)
+            nc.vector.tensor_tensor(y[:, t, cols], o_bank[:], picked_me[t][:, cols], MULT)
 
         def quantise_values(t, vals_grouped):
             return quantise(f"vals{t}", vals_grouped[:], P)
 
-        vals0 = quantise_values(0, turn_values(0, gather_values(0)))
-        vals1 = quantise_values(1, turn_values(1, gather_values(1)))
+        def look_up(t):
+            picked = tile(f"picked_me{t}", [P, J], F32, tag=f"val_pool{t - 2}" if t >= 2 else None)
+            nc.scalar.activation(picked[:], memories[t][:].indirect(idx3[:]), COPY)
+            return picked
+
+        picked_me = [look_up(0), look_up(1)]
+        picked0 = gather_values(0)
+        picked_me.append(look_up(2))
+        picked1 = gather_values(1)
+        picked_me.append(look_up(3))
+        vals0 = quantise_values(0, turn_values(0, picked0))
+        vals1 = quantise_values(1, turn_values(1, picked1))
         multiply_values(0, *vals0, "o_first")
         picked2 = gather_values(2)
         picked3 = gather_values(3)
@@ -216,11 +221,15 @@ def tile_attend_tab_plain_gains_pl_kernel(
         nc.scalar.copy(y_places[:, :, 0:2, :], y_planes[:, :, 0:2, :])
         multiply_values(2, *vals2, "shared1")
         nc.sync.dma_start(out_rows[:, 0:3, :], y[:, 0:3, :])
-        multiply_values(3, *vals3, "o_last")
+        for h in range(J // P):
+            multiply_values(3, *vals3, f"o_last{h}", slice(h * P, (h + 1) * P))
         nc.sync.dma_start(out_rows[:, 3, :], y[:, 3, :])
 
-        nc.vector.tensor_copy(y_places[:, :, 2:4, :], y_planes[:, :, 2:4, :])
-        y_codes, y_scales = quantise("y", y_grouped[:], J)
+        runs = P // PACK
+        for h in range(J // P):
+            part = slice(h * runs, (h + 1) * runs)
+            nc.vector.tensor_copy(y_places[:, part, 2:4, :], y_planes[:, part, 2:4, :])
+        y_codes, y_scales = quantise("y", y_grouped[:], J, parts=J // P)
         nc.sync.dma_start(out_1[0].rearrange("p c r -> p (c r)").bitcast(I32), y_codes[:].bitcast(I32))
         for q in range(4):
             queue = nc.scalar if q % 2 == 0 else nc.sync

@@ -66,8 +66,7 @@ def tile_attend_tab_plain_gains_pl_kernel(
         nc.vector.memset(key_bytes[:].bitcast(I32), 0)
         nc.sync.dma_start(key_words[:].bitcast(I32), keys_words[0].bitcast(I32))
         nc.sync.dma_start(idx[:], offs)
-        for r in range(4):
-            nc.sync.dma_start(key_bytes[r:P:32, :].bitcast(I32), keys_scales[0, r:16:4, :].bitcast(I32))
+        nc.sync.dma_start(key_bytes[0:P:8, :].bitcast(I32), keys_scales[0].bitcast(I32))
         nc.sync.dma_start(wm_raw[:], wm.rearrange("(p t) e -> p t e", t=PACK))
         store_rows = mstore.rearrange("(p t) m -> p t m", t=PACK)
         for h in range(M // BANK):
@@ -89,22 +88,27 @@ def tile_attend_tab_plain_gains_pl_kernel(
         nc.vector.tensor_copy(picked_words[:], key_words[:].indirect(idx[:]))
         dealt_bytes = tile("dealt_bytes", [P, PACK, P], U8)
         nc.vector.tensor_copy(dealt_bytes[:].rearrange("p t s -> p s t"), key_bytes[:].indirect(idx[:]))
+        key_plane = tile("key_plane", [P, I], U8)
+        nc.gpsimd.memset(key_plane[:].bitcast(I32), 0)
+        dealt_rows = dealt_bytes[:].rearrange("p t s -> p (t s)").bitcast(I32)
+        for q in range(4):
+            nc.gpsimd.dma_start(key_plane[32 * q : 32 * q + 4, :].bitcast(I32), dealt_rows[32 * q : 32 * q + 32 : 8, :])
         dealt_words = tile("dealt_words", [P, PACK, P], U16)
         nc.vector.tensor_copy(
             dealt_words[:].rearrange("p t s -> p s t"), picked_words[:].rearrange("p (s t) -> p s t", t=PACK)
         )
 
         wm_grouped = tile("wm_grouped", [P, E * PACK], BF16)
-        nc.vector.tensor_copy(
-            out=wm_grouped[:].rearrange("p (t s r) -> p s r t", t=PACK, r=PACK),
-            in_=wm_raw[:].rearrange("p r (s t) -> p s r t", t=PACK),
-        )
+        wm_places = wm_grouped[:].rearrange("p (t s r) -> p s r t", t=PACK, r=PACK)
+        wm_rows = wm_raw[:].rearrange("p r (s t) -> p s r t", t=PACK)
+        nc.scalar.copy(wm_places[:, : P // 2], wm_rows[:, : P // 2])
+        nc.vector.tensor_copy(wm_places[:, P // 2 :], wm_rows[:, P // 2 :])
         wm_codes, wm_scales = quantise("wm", wm_grouped[:], E)
         memories = [tile(f"memories{t}", [P, M], F32) for t in range(PACK)]
         for h in range(M // BANK):
             store_grouped = tile(f"store_grouped{h}", [P, BANK * PACK], BF16, tag="store_grouped")
             if h == 0:
-                cut = BANK // 2
+                cut = 192
                 interleave(store_grouped[:, : cut * PACK], store_raw[h][:, :, :cut], nc.scalar.copy)
                 interleave(store_grouped[:, cut * PACK :], store_raw[h][:, :, cut:])
             else:
@@ -137,7 +141,7 @@ def tile_attend_tab_plain_gains_pl_kernel(
                 nc.tensor.matmul_mx(
                     out=table_bank[:, t, :],
                     lhsT=dealt_words[:, t, :].bitcast(FP4X4),
-                    lhsT_scale=dealt_bytes[:, t, :],
+                    lhsT_scale=key_plane[:, t * P : (t + 1) * P],
                     rhs=note_codes[:, h * P : (h + 1) * P].bitcast(FP8X4),
                     rhs_scale=note_scales[:, h * P : (h + 1) * P],
                     start=True,

from contextlib import ExitStack

import concourse.mybir as mybir
from concourse.masks import make_identity

D, T, I, J, U, E, M, C = 512, 2048, 512, 256, 1024, 512, 1024, 512
FLOPS = 2 * D * I * J + 2 * I * E * J + 2 * C * E * M

F32 = mybir.dt.float32
BF16 = mybir.dt.bfloat16
I32 = mybir.dt.int32
U32 = mybir.dt.uint32
U16 = mybir.dt.uint16
U8 = mybir.dt.uint8
FP8X4 = mybir.dt.float8_e4m3fn_x4
FP4X4 = mybir.dt.float4_e2m1fn_x4
COPY = mybir.ActivationFunctionType.Copy
MULT = mybir.AluOpType.mult
MAX = mybir.AluOpType.max

P = 128
PACK = 4
BANK = 512


def tile_attend_tab_plain_gains_pl_kernel(
    tc, keys_words, keys_scales, notes, rowf, vals, wm, mstore, offs, offs2, offs3, out_0, out_1, out_2
):
    nc = tc.nc
    with ExitStack() as ctx:
        sb = ctx.enter_context(tc.tile_pool(name="sb", bufs=1))
        ps = ctx.enter_context(tc.psum_pool(name="ps", bufs=2))

        def tile(name, shape, dtype, tag=None):
            return sb.tile(shape, dtype, name=name, tag=tag or name, align_bytes=64)

        def quantise(name, grouped, width, parts=1):
            codes = tile(name + "_codes", [P, width], U32)
            scales = tile(name + "_scales", [P, width], U8)
            step = width // parts
            for c in range(0, width, step):
                nc.vector.quantize_mx(
                    out=codes[:, c : c + step].bitcast(FP8X4),
                    scales=scales[:, c : c + step],
                    in_=grouped[:, c * PACK : (c + step) * PACK],
                )
            return codes, scales

        def interleave(grouped, planes, copy=nc.vector.tensor_copy):
            copy(
                out=grouped.rearrange("p (c i t) -> p c t i", i=PACK, t=PACK),
                in_=planes.rearrange("p t (c i) -> p c t i", i=PACK),
            )

        idx = sb.tile([P, I // 16], U16, name="idx")
        idx2 = sb.tile([P, J // 16], U16, name="idx2")
        idx3 = sb.tile([P, J // 16], U16, name="idx3")
        key_words = tile("key_words", [P, T], U16)
        key_bytes = tile("key_bytes", [P, T], U8)
        row_factor = tile("row_factor", [P, PACK], F32)
        wm_raw = tile("wm_raw", [P, PACK, E], F32)
        store_raw = [tile(f"store_raw{h}", [P, PACK, BANK], F32) for h in range(M // BANK)]
        note_pool = [tile(f"note_pool{t}", [P, U], F32) for t in range(PACK)]
        val_pool = [tile(f"val_pool{t}", [P, T], F32) for t in range(PACK)]

        nc.vector.memset(key_bytes[:].bitcast(I32), 0)
        nc.sync.dma_start(key_words[:].bitcast(I32), keys_words[0].bitcast(I32))
        nc.sync.dma_start(idx[:], offs)
        nc.sync.dma_start(key_bytes[0:P:8, :].bitcast(I32), keys_scales[0].bitcast(I32))
        nc.sync.dma_start(wm_raw[:], wm.rearrange("(p t) e -> p t e", t=PACK))
        store_rows = mstore.rearrange("(p t) m -> p t m", t=PACK)
        for h in range(M // BANK):
            nc.sync.dma_start(store_raw[h][:], store_rows[:, :, h * BANK : (h + 1) * BANK])
        nc.scalar.dma_start(row_factor[:], rowf.rearrange("(p t) one -> p (t one)", t=PACK))
        nc.sync.dma_start(idx2[:], offs2)
        nc.sync.dma_start(idx3[:], offs3)
        note_rows = notes.rearrange("(p t) u -> p t u", t=PACK)
        for t in range(PACK):
            nc.sync.dma_start(note_pool[t][:], note_rows[:, t, :])
        val_rows = vals.rearrange("(p t) n -> p t n", t=PACK)
        for t in range(PACK):
            nc.sync.dma_start(val_pool[t][:], val_rows[:, t, :])

        identity = tile("identity", [P, P], F32)
        make_identity(nc, identity[:])

        picked_words = tile("picked_words", [P, I], U16)
        nc.vector.tensor_copy(picked_words[:], key_words[:].indirect(idx[:]))
        dealt_bytes = tile("dealt_bytes", [P, PACK, P], U8)
        nc.vector.tensor_copy(dealt_bytes[:].rearrange("p t s -> p s t"), key_bytes[:].indirect(idx[:]))
        key_plane = tile("key_plane", [P, I], U8)
        nc.gpsimd.memset(key_plane[:].bitcast(I32), 0)
        dealt_rows = dealt_bytes[:].rearrange("p t s -> p (t s)").bitcast(I32)
        for q in range(4):
            nc.gpsimd.dma_start(key_plane[32 * q : 32 * q + 4, :].bitcast(I32), dealt_rows[32 * q : 32 * q + 32 : 8, :])
        dealt_words = tile("dealt_words", [P, PACK, P], U16)
        nc.vector.tensor_copy(
            dealt_words[:].rearrange("p t s -> p s t"), picked_words[:].rearrange("p (s t) -> p s t", t=PACK)
        )

        wm_grouped = tile("wm_grouped", [P, E * PACK], BF16)
        wm_places = wm_grouped[:].rearrange("p (t s r) -> p s r t", t=PACK, r=PACK)
        wm_rows = wm_raw[:].rearrange("p r (s t) -> p s r t", t=PACK)
        nc.scalar.copy(wm_places[:, : P // 2], wm_rows[:, : P // 2])
        nc.vector.tensor_copy(wm_places[:, P // 2 :], wm_rows[:, P // 2 :])
        wm_codes, wm_scales = quantise("wm", wm_grouped[:], E)
        memories = [tile(f"memories{t}", [P, M], F32) for t in range(PACK)]
        for h in range(M // BANK):
            store_grouped = tile(f"store_grouped{h}", [P, BANK * PACK], BF16, tag="store_grouped")
            if h == 0:
                cut = 192
                interleave(store_grouped[:, : cut * PACK], store_raw[h][:, :, :cut], nc.scalar.copy)
                interleave(store_grouped[:, cut * PACK :], store_raw[h][:, :, cut:])
            else:
                interleave(store_grouped[:], store_raw[h][:])
            store_codes, store_scales = quantise(f"store{h}", store_grouped[:], BANK)
            for t in range(PACK):
                me_bank = ps.tile([P, BANK], F32, name="me_bank", bufs=3)
                nc.tensor.matmul_mx(
                    out=me_bank[:],
                    lhsT=wm_codes[:, t * P : (t + 1) * P].bitcast(FP8X4),
                    lhsT_scale=wm_scales[:, t * P : (t + 1) * P],
                    rhs=store_codes[:].bitcast(FP8X4),
                    rhs_scale=store_scales[:],
                    start=True,
                    stop=True,
                )
                nc.scalar.copy(memories[t][:, h * BANK : (h + 1) * BANK], me_bank[:])

        picked_notes = tile("picked_notes", [P, PACK, J], BF16, tag="store_grouped")
        for t in range(PACK):
            nc.vector.tensor_copy(picked_notes[:, t, :], note_pool[t][:].indirect(idx2[:]))
        notes_grouped = tile("notes_grouped", [P, J * PACK], BF16)
        for h in range(J // P):
            interleave(notes_grouped[:, h * P * PACK : (h + 1) * P * PACK], picked_notes[:, :, h * P : (h + 1) * P])
        note_codes, note_scales = quantise("notes", notes_grouped[:], J, parts=J // P)
        table_grouped = tile("table_grouped", [P, J * PACK], BF16)
        for h in range(J // P):
            table_bank = ps.tile([P, PACK, P], F32, name="table_bank", tag=f"shared{h}", bufs=1)
            for t in range(PACK):
                nc.tensor.matmul_mx(
                    out=table_bank[:, t, :],
                    lhsT=dealt_words[:, t, :].bitcast(FP4X4),
                    lhsT_scale=key_plane[:, t * P : (t + 1) * P],
                    rhs=note_codes[:, h * P : (h + 1) * P].bitcast(FP8X4),
                    rhs_scale=note_scales[:, h * P : (h + 1) * P],
                    start=True,
                    stop=True,
                )
            nc.vector.scalar_tensor_tensor(
                out=table_grouped[:, h * P * PACK : (h + 1) * P * PACK].rearrange("p (j t) -> p j t", t=PACK),
                in0=table_bank[:].rearrange("p t j -> p j t"),
                scalar=0.0,
                in1=row_factor[:].unsqueeze(1).to_broadcast([P, P, PACK]),
                op0=MAX,
                op1=MULT,
            )
        table_codes, table_scales = quantise("table", table_grouped[:], J, parts=J // P)

        def gather_values(t):
            picked_vals = tile(f"picked_vals{t}", [P, I], BF16, tag=("memories1", "memories2", "memories3", "vals_grouped1")[t])
            if t < PACK - 1:
                nc.scalar.activation(picked_vals[:], val_pool[t][:].indirect(idx[:]), COPY)
            else:
                half, cols = I // 2, I // 32
                nc.scalar.activation(picked_vals[:, :half], val_pool[t][:].indirect(idx[:, :cols]), COPY)
                nc.vector.tensor_copy(picked_vals[:, half:], val_pool[t][:].indirect(idx[:, cols:]))
            return picked_vals

        def turn_values(t, picked_vals):
            pairs = picked_vals[:].bitcast(F32)
            turn_bank = ps.tile([P, 2, P], F32, name="turn_bank", tag=f"shared{t % 2}", bufs=1)
            for u in range(2):
                nc.tensor.transpose(turn_bank[:, u, :], pairs[:, u : I // 2 : 2], identity[:])
            vals_grouped = tile(f"vals_grouped{t}", [P, P * PACK], BF16, tag="val_pool3" if t == 2 else None)
            leave_bank = nc.vector.tensor_copy if t < PACK - 1 else nc.scalar.copy
            leave_bank(
                vals_grouped[:].bitcast(F32).rearrange("p (e u) -> p e u", u=2),
                turn_bank[:].rearrange("p u e -> p e u"),
            )
            return vals_grouped

        y = tile("y", [P, PACK, J], F32)
        out_rows = out_0.rearrange("(p t) j -> p t j", t=PACK)
        y_grouped = tile("y_grouped", [P, J * PACK], BF16)
        y_places = y_grouped[:].rearrange("p (c i t) -> p c t i", i=PACK, t=PACK)
        y_planes = y[:].rearrange("p t (c i) -> p c t i", i=PACK)

        def multiply_values(t, val_codes, val_scales, bank_tag, cols=slice(0, J)):
            o_bank = ps.tile([P, cols.stop - cols.start], F32, name="o_bank", tag=bank_tag, bufs=1)
            nc.tensor.matmul_mx(
                out=o_bank[:],
                lhsT=val_codes[:].bitcast(FP8X4),
                lhsT_scale=val_scales[:],
                rhs=table_codes[:, cols].bitcast(FP8X4),
                rhs_scale=table_scales[:, cols],
                start=True,
                stop=True,
            )
            nc.vector.tensor_tensor(y[:, t, cols], o_bank[:], picked_me[t][:, cols], MULT)

        def quantise_values(t, vals_grouped):
            return quantise(f"vals{t}", vals_grouped[:], P)

        def look_up(t):
            picked = tile(f"picked_me{t}", [P, J], F32, tag=f"val_pool{t - 2}" if t >= 2 else None)
            nc.scalar.activation(picked[:], memories[t][:].indirect(idx3[:]), COPY)
            return picked

        picked_me = [look_up(0), look_up(1)]
        picked0 = gather_values(0)
        picked_me.append(look_up(2))
        picked1 = gather_values(1)
        picked_me.append(look_up(3))
        vals0 = quantise_values(0, turn_values(0, picked0))
        vals1 = quantise_values(1, turn_values(1, picked1))
        multiply_values(0, *vals0, "o_first")
        picked2 = gather_values(2)
        picked3 = gather_values(3)
        grouped2 = turn_values(2, picked2)
        grouped3 = turn_values(3, picked3)
        vals2 = quantise_values(2, grouped2)
        vals3 = quantise_values(3, grouped3)
        multiply_values(1, *vals1, "shared0")
        nc.scalar.copy(y_places[:, :, 0:2, :], y_planes[:, :, 0:2, :])
        multiply_values(2, *vals2, "shared1")
        nc.sync.dma_start(out_rows[:, 0:3, :], y[:, 0:3, :])
        for h in range(J // P):
            multiply_values(3, *vals3, f"o_last{h}", slice(h * P, (h + 1) * P))
        nc.sync.dma_start(out_rows[:, 3, :], y[:, 3, :])

        runs = P // PACK
        for h in range(J // P):
            part = slice(h * runs, (h + 1) * runs)
            nc.vector.tensor_copy(y_places[:, part, 2:4, :], y_planes[:, part, 2:4, :])
        y_codes, y_scales = quantise("y", y_grouped[:], J, parts=J // P)
        nc.sync.dma_start(out_1[0].rearrange("p c r -> p (c r)").bitcast(I32), y_codes[:].bitcast(I32))
        for q in range(4):
            queue = nc.scalar if q % 2 == 0 else nc.sync
            queue.dma_start(out_2[0, 4 * q : 4 * q + 4, :].bitcast(I32), y_scales[32 * q : 32 * q + 4, :].bitcast(I32))
